import numpy as np
import ml_dtypes


def mxq(x, axis, fmt="e4m3"):
    dtype, down = {"e4m3": (ml_dtypes.float8_e4m3fn, 7), "e5m2": (ml_dtypes.float8_e5m2, 14)}[fmt]
    v = np.moveaxis(np.asarray(x, np.float32).astype(ml_dtypes.bfloat16).astype(np.float64), axis, -1)
    blocks = v.reshape(v.shape[:-1] + (-1, 32))
    amax = np.abs(blocks).max(-1, keepdims=True)
    byte = np.maximum(np.where(amax > 0, np.frexp(amax)[1] - 1 + 127, 0) - down, 1)
    scale = np.exp2(byte - 127.0)
    codes = (blocks / scale).astype(np.float32).astype(dtype).astype(np.float64)
    return np.moveaxis((codes * scale).reshape(v.shape), -1, axis)


WIDE = False


def mx_kscale(k):
    if not WIDE:
        return np.ones(k)
    levels = np.array([30, -30])
    if k % 512:
        return np.exp2(np.random.permutation(np.resize(levels, k // 32))).repeat(32)
    a = np.empty((k // 512, 16))
    for p in range(k // 512):
        a[p, :8] = np.random.permutation(np.resize(levels, 8))
        for g in range(8):
            far = levels[np.abs(levels - a[p, g]) >= 10]
            a[p, g + 8] = far[np.random.randint(len(far))]
    return np.exp2(a.ravel()).repeat(32)


def f64(x):
    return np.asarray(x).astype(np.float64)


def striped(idx):
    return np.tile(np.asarray(idx).reshape(-1, 16).T, (8, 1)).astype(np.uint16)


def unstriped(offs):
    return offs[:16].T.reshape(-1).astype(np.int64)


E2M1 = np.array([0.0, 0.5, 1.0, 1.5, 2.0, 3.0, 4.0, 6.0, -0.0, -0.5, -1.0, -1.5, -2.0, -3.0, -4.0, -6.0])


def pack_weight(w, fmt):
    k, n = w.shape
    w = f64(np.asarray(w, np.float32).astype(ml_dtypes.bfloat16)).reshape(k // 32, 32, n)
    amax = np.abs(w).max(1)
    if fmt == "e4m3":
        byte = np.frexp(amax)[1] - 1 + 127 - 7
    else:
        mant, ex = np.frexp(amax / 6.0)
        byte = np.where(mant > 0.5, ex, ex - 1) + 127
    byte = np.clip(np.where(amax > 0, byte, 1), 1, 254)
    scaled = (w * np.exp2(127.0 - byte)[:, None, :]).reshape(k, n).astype(np.float32)
    by_word = np.ascontiguousarray(scaled.reshape(k // 512, 128, 4, n).transpose(0, 1, 3, 2))
    if fmt == "e4m3":
        words = by_word.astype(ml_dtypes.float8_e4m3fn).view(np.uint8)
    else:
        c = by_word.astype(ml_dtypes.float4_e2m1fn).view(np.uint8) & 0xF
        words = (c[..., 0::2] | (c[..., 1::2] << 4)).reshape(k // 512, 128, 2 * n)
    return np.ascontiguousarray(words), np.ascontiguousarray(byte.astype(np.uint8).reshape(k // 512, 16, n))


def unpack_weight(words, scales, fmt):
    g, _, n = scales.shape
    words = np.ascontiguousarray(words).reshape(g, 128, n, -1)
    if fmt == "e4m3":
        vals = words.view(ml_dtypes.float8_e4m3fn).astype(np.float64)
    else:
        nib = np.empty((g, 128, n, 4), np.uint8)
        nib[..., 0::2] = words & 0xF
        nib[..., 1::2] = words >> 4
        vals = E2M1[nib]
    vals = vals * np.repeat(np.exp2(scales.astype(np.float64) - 127.0), 8, axis=1)[..., None]
    return vals.transpose(0, 1, 3, 2).reshape(g * 512, n)


K, T, J, R, Q, N, E = 512, 2048, 256, 512, 1024, 256, 128


def setup_inputs():
    n = np.random.standard_normal
    idx = np.random.permutation(T)[:J]
    idx2 = np.random.permutation(T)[:J]
    idx3 = np.random.permutation(Q)[:J]
    idx4 = np.random.permutation(J)[:E]
    idx5 = np.random.permutation(J)[:E]
    fk = mx_kscale(K)
    fr = mx_kscale(R)
    xtp = pack_weight(n((K, T)) / fk[:, None], "e2m1")
    wp = pack_weight(n((K, R)) * 1 / np.sqrt(K) * fk[:, None] * fr, "e4m3")
    wbp = pack_weight(n((R, N)) * 1 / np.sqrt(R) / fr[:, None], "e2m1")
    wsp = pack_weight(n((K, N)) * 1 / np.sqrt(K) * fk[:, None], "e4m3")
    return {
        "xt_words": xtp[0],
        "xt_scales": xtp[1],
        "w_words": wp[0],
        "w_scales": wp[1],
        "ta": (np.random.uniform(-2.0, 1.0, (R, Q))).astype(np.float32),
        "wb_words": wbp[0],
        "wb_scales": wbp[1],
        "ws_words": wsp[0],
        "ws_scales": wsp[1],
        "offs": striped(idx),
        "offs2": striped(idx2),
        "offs3": striped(idx3),
        "offs4": striped(idx4),
        "offs5": striped(idx5),
    }


def reference(xt_words, xt_scales, w_words, w_scales, ta, wb_words, wb_scales, ws_words, ws_scales, offs, offs2, offs3, offs4, offs5):
    idx = unstriped(offs)
    idx2 = unstriped(offs2)
    idx3 = unstriped(offs3)
    idx4 = unstriped(offs4)
    idx5 = unstriped(offs5)
    xtu = unpack_weight(xt_words, xt_scales, "e2m1")
    wu = unpack_weight(w_words, w_scales, "e4m3")
    wbu = unpack_weight(wb_words, wb_scales, "e2m1")
    wsu = unpack_weight(ws_words, ws_scales, "e4m3")
    xtidxg = xtu[:, idx]
    a = wu.T @ xtidxg
    xtidx2g = xtu[:, idx2]
    b = wu.T @ xtidx2g
    nm = -np.max(f64(ta), axis=1, keepdims=True)
    hid = np.abs(a - b) * np.exp(f64(ta)[:, idx3] + nm)
    hidq = mxq(hid, 0, "e5m2")
    p = wbu.T @ hidq + wsu.T @ xtidxg
    y = np.maximum(p[:, idx4], p[:, idx5])
    return y

@@ -1,0 +1,194 @@
+from contextlib import ExitStack
+
+import concourse.mybir as mybir
+
+K, T, J, R, Q, N, E = 512, 2048, 256, 512, 1024, 256, 128
+FLOPS = 2 * K * R * J * 2 + 2 * R * N * J + 2 * K * N * J
+
+F32 = mybir.dt.float32
+BF16 = mybir.dt.bfloat16
+I32 = mybir.dt.int32
+U32 = mybir.dt.uint32
+U16 = mybir.dt.uint16
+U8 = mybir.dt.uint8
+E2M1X4 = mybir.dt.float4_e2m1fn_x4
+E4M3X4 = mybir.dt.float8_e4m3fn_x4
+E5M2X4 = mybir.dt.float8_e5m2_x4
+ALU = mybir.AluOpType
+ACT = mybir.ActivationFunctionType
+
+P = 128
+PACK = 4
+H = J // 2
+
+
+def load_scale_rows(queue, plane, rows, quads=(0, 1, 2, 3)):
+    for quad in quads:
+        queue.dma_start(
+            out=plane[32 * quad : 32 * quad + 4, :].bitcast(I32),
+            in_=rows[0, 4 * quad : 4 * quad + 4, :].bitcast(I32),
+        )
+
+
+def tile_list_tied_fading_skip_bestoftwo_kernel(
+    tc, xt_words, xt_scales, w_words, w_scales, ta, wb_words, wb_scales, ws_words, ws_scales,
+    offs, offs2, offs3, offs4, offs5, out,
+):
+    nc = tc.nc
+    with ExitStack() as ctx:
+        sb = ctx.enter_context(tc.tile_pool(name="sb", bufs=1))
+        ps = ctx.enter_context(tc.psum_pool(name="ps", bufs=1))
+
+        list1 = sb.tile([P, J // 16], U16, name="list1")
+        list2 = sb.tile([P, J // 16], U16, name="list2")
+        list3 = sb.tile([P, J // 16], U16, name="list3")
+        list4 = sb.tile([P, E // 16], U16, name="list4")
+        list5 = sb.tile([P, E // 16], U16, name="list5")
+        x_words = sb.tile([P, T], U16, name="x_words")
+        x_plane = sb.tile([P, T], U8, name="x_plane")
+        w_raw = sb.tile([P, R], U32, name="w_raw")
+        w_raw_plane = sb.tile([P, R], U8, name="w_raw_plane")
+        w_dealt = sb.tile([P, R], U32, name="w_dealt", align_bytes=64)
+        w_plane = sb.tile([P, R], U8, name="w_plane", align_bytes=64)
+        ws_codes = sb.tile([P, N], U32, name="ws_codes", align_bytes=64)
+        wb_codes = sb.tile([P, 2 * N], U8, name="wb_codes", align_bytes=64)
+        ws_plane = sb.tile([P, N], U8, name="ws_plane", align_bytes=64)
+        wb_plane = sb.tile([P, N], U8, name="wb_plane", align_bytes=64)
+        levels = [sb.tile([P, Q], F32, name="levels%d" % t) for t in range(PACK)]
+        neg_top = [sb.tile([P, 1], F32, name="neg_top%d" % t) for t in range(PACK)]
+        picked = sb.tile([P, 2 * J], U16, name="picked", align_bytes=64)
+        picked_plane = sb.tile([P, 2 * J], U8, name="picked_plane", align_bytes=64)
+
+        nc.vector.memset(x_plane[:, 0 : T // 2].bitcast(I32), 0)
+        nc.gpsimd.memset(x_plane[:, T // 2 : T].bitcast(I32), 0)
+        nc.vector.memset(w_raw_plane[:].bitcast(I32), 0)
+        nc.gpsimd.memset(ws_plane[:].bitcast(I32), 0)
+        nc.gpsimd.memset(wb_plane[:].bitcast(I32), 0)
+
+        ta_rows = ta.rearrange("(p t) q -> p t q", t=PACK)
+        nc.sync.dma_start(list2[:], offs2)
+        nc.sync.dma_start(list1[:], offs)
+        nc.sync.dma_start(out=x_words[:].bitcast(I32), in_=xt_words[0].bitcast(I32))
+        load_scale_rows(nc.scalar, x_plane, xt_scales)
+        nc.sync.dma_start(out=levels[0][:], in_=ta_rows[:, 0, :])
+        nc.sync.dma_start(out=w_raw[:].bitcast(I32), in_=w_words[0].rearrange("p n t -> p (n t)").bitcast(I32))
+        load_scale_rows(nc.scalar, w_raw_plane, w_scales, (0, 1))
+        load_scale_rows(nc.gpsimd, w_raw_plane, w_scales, (2, 3))
+        nc.sync.dma_start(list3[:], offs3)
+        for t in range(1, PACK):
+            nc.sync.dma_start(out=levels[t][:], in_=ta_rows[:, t, :])
+        load_scale_rows(nc.sync, ws_plane, ws_scales)
+        nc.sync.dma_start(out=ws_codes[:].bitcast(I32), in_=ws_words[0].rearrange("p n t -> p (n t)").bitcast(I32))
+        nc.sync.dma_start(out=wb_codes[:].bitcast(I32), in_=wb_words[0].bitcast(I32))
+        load_scale_rows(nc.sync, wb_plane, wb_scales)
+        nc.sync.dma_start(list4[:], offs4)
+        nc.sync.dma_start(list5[:], offs5)
+
+        nc.vector.tensor_copy(picked_plane[:, 0:J], x_plane[:].indirect(list2[:]))
+        nc.vector.tensor_copy(picked_plane[:, J : 2 * J], x_plane[:].indirect(list1[:]))
+        nc.vector.tensor_copy(picked[:, 0:J], x_words[:].indirect(list2[:]))
+        nc.vector.tensor_copy(picked[:, J : 2 * J], x_words[:].indirect(list1[:]))
+
+        nc.scalar.copy(
+            out=w_dealt[:].rearrange("p (t c i) -> p c t i", t=PACK, i=4),
+            in_=w_raw[:].rearrange("p (c i t) -> p c t i", t=PACK, i=4),
+        )
+        nc.gpsimd.tensor_copy(
+            out=w_plane[:].rearrange("p (t c i) -> p c t i", t=PACK, i=16),
+            in_=w_raw_plane[:].rearrange("p (c i t) -> p c t i", t=PACK, i=16),
+        )
+
+        first = [ps.tile([P, 2 * J], F32, name="first%d" % t) for t in range(PACK)]
+        for t in range(PACK):
+            nc.tensor.matmul_mx(
+                out=first[t][:],
+                lhsT=w_dealt[:, t * P : (t + 1) * P].bitcast(E4M3X4),
+                lhsT_scale=w_plane[:, t * P : (t + 1) * P],
+                rhs=picked[:].bitcast(E2M1X4),
+                rhs_scale=picked_plane[:],
+                start=True,
+                stop=True,
+            )
+        second = [ps.tile([P, J], F32, name="second%d" % h) for h in range(2)]
+        for h in range(2):
+            nc.tensor.matmul_mx(
+                out=second[h][:],
+                lhsT=ws_codes[:, h * P : (h + 1) * P].bitcast(E4M3X4),
+                lhsT_scale=ws_plane[:, h * P : (h + 1) * P],
+                rhs=picked[:, J : 2 * J].bitcast(E2M1X4),
+                rhs_scale=picked_plane[:, J : 2 * J],
+                start=True,
+                stop=False,
+            )
+
+        WID = J
+        moved = sb.tile([P, PACK, WID], F32, name="moved")
+        fade = sb.tile([P, PACK, J], F32, name="fade")
+        diff_a = sb.tile([P, PACK, H], F32, name="diff_a")
+        mag_a = sb.tile([P, PACK, H], F32, name="mag_a")
+        diff_b = sb.tile([P, PACK, H], F32, name="diff_b")
+        prod_b = sb.tile([P, PACK, H], F32, name="prod_b")
+        hid = [sb.tile([P, PACK * H], BF16, name="hid%d" % u, align_bytes=64) for u in range(2)]
+        hid_codes = [sb.tile([P, H], U32, name="hid_codes%d" % u, align_bytes=64) for u in range(2)]
+        hid_plane = [sb.tile([P, H], U8, name="hid_plane%d" % u, align_bytes=64) for u in range(2)]
+
+        def top(t):
+            nc.vector.tensor_reduce(
+                out=neg_top[t][:], in_=levels[t][:], axis=mybir.AxisListType.X, op=ALU.max, negate=True
+            )
+
+        def look(t):
+            nc.scalar.activation(out=fade[:, t, :], in_=levels[t][:].indirect(list3[:]), func=ACT.Exp, bias=neg_top[t][:])
+
+        for t in range(PACK):
+            nc.scalar.copy(out=moved[:, t, :], in_=first[t][:, 0:WID])
+        for t in range(PACK - 1):
+            top(t)
+            look(t)
+        for t in range(PACK):
+            nc.vector.tensor_tensor(out=diff_a[:, t, :], in0=first[t][:, J : J + H], in1=moved[:, t, 0:H], op=ALU.subtract)
+        nc.scalar.activation(out=mag_a[:], in_=diff_a[:], func=ACT.Abs)
+        top(PACK - 1)
+        look(PACK - 1)
+        for t in range(PACK):
+            nc.vector.tensor_tensor(out=diff_b[:, t, :], in0=first[t][:, J + H : 2 * J], in1=moved[:, t, H:J], op=ALU.subtract)
+        nc.vector.tensor_tensor(out=prod_b[:, 0:3, :], in0=diff_b[:, 0:3, :], in1=fade[:, 0:3, H:J], op=ALU.mult)
+        nc.vector.tensor_tensor(out=prod_b[:, 3, :], in0=diff_b[:, 3, :], in1=fade[:, 3, H:J], op=ALU.mult)
+        nc.vector.tensor_tensor(
+            out=hid[0][:].rearrange("p (c i t) -> p c t i", t=PACK, i=2),
+            in0=mag_a[:].rearrange("p t (c i) -> p c t i", i=2),
+            in1=fade[:, :, 0:H].rearrange("p t (c i) -> p c t i", i=2),
+            op=ALU.mult,
+        )
+        nc.scalar.activation(
+            out=hid[1][:].rearrange("p (c i t) -> p c t i", t=PACK, i=2),
+            in_=prod_b[:].rearrange("p t (c i) -> p c t i", i=2),
+            func=ACT.Abs,
+        )
+        for u in range(2):
+            nc.vector.quantize_mx(out=hid_codes[u][:].bitcast(E5M2X4), scales=hid_plane[u][:], in_=hid[u][:])
+        for u in range(2):
+            for h in range(2):
+                nc.tensor.matmul_mx(
+                    out=second[h][:, u * H : (u + 1) * H],
+                    lhsT=wb_codes[:, 2 * h * P : 2 * (h + 1) * P].bitcast(E2M1X4),
+                    lhsT_scale=wb_plane[:, h * P : (h + 1) * P],
+                    rhs=hid_codes[u][:].bitcast(E5M2X4),
+                    rhs_scale=hid_plane[u][:],
+                    start=False,
+                    stop=(u == 1),
+                )
+
+        whole = [sb.tile([P, J], F32, name="whole%d" % h) for h in range(2)]
+        left = [sb.tile([P, E], F32, name="left%d" % h) for h in range(2)]
+        right = [sb.tile([P, E], F32, name="right%d" % h) for h in range(2)]
+        best = [sb.tile([P, E], F32, name="best%d" % h) for h in range(2)]
+        nc.vector.tensor_copy(out=whole[0][:], in_=second[0][:])
+        nc.scalar.copy(out=whole[1][:], in_=second[1][:])
+        nc.vector.tensor_copy(left[0][:], whole[0][:].indirect(list4[:]))
+        nc.scalar.activation(out=left[1][:], in_=whole[1][:].indirect(list4[:]), func=ACT.Copy)
+        nc.vector.tensor_copy(right[0][:], whole[0][:].indirect(list5[:]))
+        nc.scalar.activation(out=right[1][:], in_=whole[1][:].indirect(list5[:]), func=ACT.Copy)
+        for h in range(2):
+            nc.vector.tensor_tensor(out=best[h][:], in0=left[h][:], in1=right[h][:], op=ALU.max)
+            (nc.sync, nc.scalar)[h].dma_start(out=out[h * P : (h + 1) * P, :], in_=best[h][:])

@@ -54,7 +54,7 @@ def tile_list_tied_fading_skip_bestoftwo_kernel(
         wb_codes = sb.tile([P, 2 * N], U8, name="wb_codes", align_bytes=64)
         ws_plane = sb.tile([P, N], U8, name="ws_plane", align_bytes=64)
         wb_plane = sb.tile([P, N], U8, name="wb_plane", align_bytes=64)
-        levels = [sb.tile([P, Q], F32, name="levels%d" % t) for t in range(PACK)]
+        levels = [sb.tile([P, Q], F32, name="levels%d" % t, tag="levels%d" % t) for t in range(PACK)]
         neg_top = [sb.tile([P, 1], F32, name="neg_top%d" % t) for t in range(PACK)]
         picked = sb.tile([P, 2 * J], U16, name="picked", align_bytes=64)
         picked_plane = sb.tile([P, 2 * J], U8, name="picked_plane", align_bytes=64)
@@ -67,15 +67,15 @@ def tile_list_tied_fading_skip_bestoftwo_kernel(
 
         ta_rows = ta.rearrange("(p t) q -> p t q", t=PACK)
         nc.sync.dma_start(list2[:], offs2)
-        nc.sync.dma_start(list1[:], offs)
         nc.sync.dma_start(out=x_words[:].bitcast(I32), in_=xt_words[0].bitcast(I32))
-        load_scale_rows(nc.scalar, x_plane, xt_scales)
-        nc.sync.dma_start(out=levels[0][:], in_=ta_rows[:, 0, :])
+        nc.sync.dma_start(list1[:], offs)
+        load_scale_rows(nc.sync, x_plane, xt_scales)
         nc.sync.dma_start(out=w_raw[:].bitcast(I32), in_=w_words[0].rearrange("p n t -> p (n t)").bitcast(I32))
-        load_scale_rows(nc.scalar, w_raw_plane, w_scales, (0, 1))
-        load_scale_rows(nc.gpsimd, w_raw_plane, w_scales, (2, 3))
+        nc.sync.dma_start(out=levels[0][:], in_=ta_rows[:, 0, :])
         nc.sync.dma_start(list3[:], offs3)
-        for t in range(1, PACK):
+        load_scale_rows(nc.sync, w_raw_plane, w_scales)
+        nc.sync.dma_start(out=levels[1][:], in_=ta_rows[:, 1, :])
+        for t in range(2, PACK):
             nc.sync.dma_start(out=levels[t][:], in_=ta_rows[:, t, :])
         load_scale_rows(nc.sync, ws_plane, ws_scales)
         nc.sync.dma_start(out=ws_codes[:].bitcast(I32), in_=ws_words[0].rearrange("p n t -> p (n t)").bitcast(I32))
@@ -93,10 +93,11 @@ def tile_list_tied_fading_skip_bestoftwo_kernel(
             out=w_dealt[:].rearrange("p (t c i) -> p c t i", t=PACK, i=4),
             in_=w_raw[:].rearrange("p (c i t) -> p c t i", t=PACK, i=4),
         )
-        nc.gpsimd.tensor_copy(
-            out=w_plane[:].rearrange("p (t c i) -> p c t i", t=PACK, i=16),
-            in_=w_raw_plane[:].rearrange("p (c i t) -> p c t i", t=PACK, i=16),
-        )
+        for pair in range(2):
+            nc.gpsimd.tensor_copy(
+                out=w_plane[:].rearrange("p (t c i) -> p c t i", t=PACK, i=16)[:, :, 2 * pair : 2 * pair + 2, :],
+                in_=w_raw_plane[:].rearrange("p (c i t) -> p c t i", t=PACK, i=16)[:, :, 2 * pair : 2 * pair + 2, :],
+            )
 
         first = [ps.tile([P, 2 * J], F32, name="first%d" % t) for t in range(PACK)]
         for t in range(PACK):
@@ -109,25 +110,23 @@ def tile_list_tied_fading_skip_bestoftwo_kernel(
                 start=True,
                 stop=True,
             )
-        second = [ps.tile([P, J], F32, name="second%d" % h) for h in range(2)]
-        for h in range(2):
-            nc.tensor.matmul_mx(
-                out=second[h][:],
-                lhsT=ws_codes[:, h * P : (h + 1) * P].bitcast(E4M3X4),
-                lhsT_scale=ws_plane[:, h * P : (h + 1) * P],
-                rhs=picked[:, J : 2 * J].bitcast(E2M1X4),
-                rhs_scale=picked_plane[:, J : 2 * J],
-                start=True,
-                stop=False,
-            )
+        second = [[ps.tile([P, H], F32, name="second%d%d" % (u, h)) for h in range(2)] for u in range(2)]
+        for u in range(2):
+            for h in range(2):
+                nc.tensor.matmul_mx(
+                    out=second[u][h][:],
+                    lhsT=ws_codes[:, h * P : (h + 1) * P].bitcast(E4M3X4),
+                    lhsT_scale=ws_plane[:, h * P : (h + 1) * P],
+                    rhs=picked[:, J + u * H : J + (u + 1) * H].bitcast(E2M1X4),
+                    rhs_scale=picked_plane[:, J + u * H : J + (u + 1) * H],
+                    start=True,
+                    stop=False,
+                )
 
-        WID = J
-        moved = sb.tile([P, PACK, WID], F32, name="moved")
+        moved = sb.tile([P, PACK, J], F32, name="moved")
         fade = sb.tile([P, PACK, J], F32, name="fade")
-        diff_a = sb.tile([P, PACK, H], F32, name="diff_a")
-        mag_a = sb.tile([P, PACK, H], F32, name="mag_a")
-        diff_b = sb.tile([P, PACK, H], F32, name="diff_b")
-        prod_b = sb.tile([P, PACK, H], F32, name="prod_b")
+        diff = [sb.tile([P, PACK, H], F32, name="diff0"), sb.tile([P, PACK, H], F32, name="diff1", tag="levels2")]
+        mag = [sb.tile([P, PACK, H], F32, name="mag%d" % u) for u in range(2)]
         hid = [sb.tile([P, PACK * H], BF16, name="hid%d" % u, align_bytes=64) for u in range(2)]
         hid_codes = [sb.tile([P, H], U32, name="hid_codes%d" % u, align_bytes=64) for u in range(2)]
         hid_plane = [sb.tile([P, H], U8, name="hid_plane%d" % u, align_bytes=64) for u in range(2)]
@@ -140,55 +139,57 @@ def tile_list_tied_fading_skip_bestoftwo_kernel(
         def look(t):
             nc.scalar.activation(out=fade[:, t, :], in_=levels[t][:].indirect(list3[:]), func=ACT.Exp, bias=neg_top[t][:])
 
+        def magnitude(u):
+            for t in range(PACK):
+                nc.vector.tensor_tensor(
+                    out=diff[u][:, t, :],
+                    in0=first[t][:, J + u * H : J + (u + 1) * H],
+                    in1=moved[:, t, u * H : (u + 1) * H],
+                    op=ALU.subtract,
+                )
+            nc.scalar.activation(out=mag[u][:], in_=diff[u][:], func=ACT.Abs)
+
         for t in range(PACK):
-            nc.scalar.copy(out=moved[:, t, :], in_=first[t][:, 0:WID])
+            nc.scalar.copy(out=moved[:, t, :], in_=first[t][:, 0:J])
         for t in range(PACK - 1):
             top(t)
             look(t)
-        for t in range(PACK):
-            nc.vector.tensor_tensor(out=diff_a[:, t, :], in0=first[t][:, J : J + H], in1=moved[:, t, 0:H], op=ALU.subtract)
-        nc.scalar.activation(out=mag_a[:], in_=diff_a[:], func=ACT.Abs)
+        magnitude(0)
         top(PACK - 1)
         look(PACK - 1)
-        for t in range(PACK):
-            nc.vector.tensor_tensor(out=diff_b[:, t, :], in0=first[t][:, J + H : 2 * J], in1=moved[:, t, H:J], op=ALU.subtract)
-        nc.vector.tensor_tensor(out=prod_b[:, 0:3, :], in0=diff_b[:, 0:3, :], in1=fade[:, 0:3, H:J], op=ALU.mult)
-        nc.vector.tensor_tensor(out=prod_b[:, 3, :], in0=diff_b[:, 3, :], in1=fade[:, 3, H:J], op=ALU.mult)
-        nc.vector.tensor_tensor(
-            out=hid[0][:].rearrange("p (c i t) -> p c t i", t=PACK, i=2),
-            in0=mag_a[:].rearrange("p t (c i) -> p c t i", i=2),
-            in1=fade[:, :, 0:H].rearrange("p t (c i) -> p c t i", i=2),
-            op=ALU.mult,
-        )
-        nc.scalar.activation(
-            out=hid[1][:].rearrange("p (c i t) -> p c t i", t=PACK, i=2),
-            in_=prod_b[:].rearrange("p t (c i) -> p c t i", i=2),
-            func=ACT.Abs,
-        )
+        magnitude(1)
+        for u in range(2):
+            nc.vector.tensor_tensor(
+                out=hid[u][:].rearrange("p (c i t) -> p c t i", t=PACK, i=2),
+                in0=mag[u][:].rearrange("p t (c i) -> p c t i", i=2),
+                in1=fade[:, :, u * H : (u + 1) * H].rearrange("p t (c i) -> p c t i", i=2),
+                op=ALU.mult,
+            )
         for u in range(2):
             nc.vector.quantize_mx(out=hid_codes[u][:].bitcast(E5M2X4), scales=hid_plane[u][:], in_=hid[u][:])
+        whole = [sb.tile([P, J], F32, name="whole%d" % h) for h in range(2)]
         for u in range(2):
             for h in range(2):
                 nc.tensor.matmul_mx(
-                    out=second[h][:, u * H : (u + 1) * H],
+                    out=second[u][h][:],
                     lhsT=wb_codes[:, 2 * h * P : 2 * (h + 1) * P].bitcast(E2M1X4),
                     lhsT_scale=wb_plane[:, h * P : (h + 1) * P],
                     rhs=hid_codes[u][:].bitcast(E5M2X4),
                     rhs_scale=hid_plane[u][:],
                     start=False,
-                    stop=(u == 1),
+                    stop=True,
                 )
+        for h in range(2):
+            nc.scalar.copy(out=whole[h][:, 0:H], in_=second[0][h][:])
+        nc.vector.tensor_copy(out=whole[0][:, H:J], in_=second[1][0][:])
+        nc.scalar.copy(out=whole[1][:, H:J], in_=second[1][1][:])
 
-        whole = [sb.tile([P, J], F32, name="whole%d" % h) for h in range(2)]
         left = [sb.tile([P, E], F32, name="left%d" % h) for h in range(2)]
         right = [sb.tile([P, E], F32, name="right%d" % h) for h in range(2)]
         best = [sb.tile([P, E], F32, name="best%d" % h) for h in range(2)]
-        nc.vector.tensor_copy(out=whole[0][:], in_=second[0][:])
-        nc.scalar.copy(out=whole[1][:], in_=second[1][:])
-        nc.vector.tensor_copy(left[0][:], whole[0][:].indirect(list4[:]))
-        nc.scalar.activation(out=left[1][:], in_=whole[1][:].indirect(list4[:]), func=ACT.Copy)
-        nc.vector.tensor_copy(right[0][:], whole[0][:].indirect(list5[:]))
-        nc.scalar.activation(out=right[1][:], in_=whole[1][:].indirect(list5[:]), func=ACT.Copy)
+        for h in range(2):
+            nc.vector.tensor_copy(left[h][:], whole[h][:].indirect(list4[:]))
+            nc.scalar.activation(out=right[h][:], in_=whole[h][:].indirect(list5[:]), func=ACT.Copy)
         for h in range(2):
             nc.vector.tensor_tensor(out=best[h][:], in0=left[h][:], in1=right[h][:], op=ALU.max)
             (nc.sync, nc.scalar)[h].dma_start(out=out[h * P : (h + 1) * P, :], in_=best[h][:])

@@ -84,32 +84,33 @@ def tile_list_tied_fading_skip_bestoftwo_kernel(
         nc.sync.dma_start(list4[:], offs4)
         nc.sync.dma_start(list5[:], offs5)
 
-        nc.vector.tensor_copy(picked_plane[:, 0:J], x_plane[:].indirect(list2[:]))
-        nc.vector.tensor_copy(picked_plane[:, J : 2 * J], x_plane[:].indirect(list1[:]))
         nc.vector.tensor_copy(picked[:, 0:J], x_words[:].indirect(list2[:]))
         nc.vector.tensor_copy(picked[:, J : 2 * J], x_words[:].indirect(list1[:]))
+        nc.vector.tensor_copy(picked_plane[:, 0:J], x_plane[:].indirect(list2[:]))
+        nc.vector.tensor_copy(picked_plane[:, J : 2 * J], x_plane[:].indirect(list1[:]))
 
-        nc.scalar.copy(
-            out=w_dealt[:].rearrange("p (t c i) -> p c t i", t=PACK, i=4),
-            in_=w_raw[:].rearrange("p (c i t) -> p c t i", t=PACK, i=4),
-        )
         for pair in range(2):
             nc.gpsimd.tensor_copy(
                 out=w_plane[:].rearrange("p (t c i) -> p c t i", t=PACK, i=16)[:, :, 2 * pair : 2 * pair + 2, :],
                 in_=w_raw_plane[:].rearrange("p (c i t) -> p c t i", t=PACK, i=16)[:, :, 2 * pair : 2 * pair + 2, :],
             )
-
-        first = [ps.tile([P, 2 * J], F32, name="first%d" % t) for t in range(PACK)]
-        for t in range(PACK):
-            nc.tensor.matmul_mx(
-                out=first[t][:],
-                lhsT=w_dealt[:, t * P : (t + 1) * P].bitcast(E4M3X4),
-                lhsT_scale=w_plane[:, t * P : (t + 1) * P],
-                rhs=picked[:].bitcast(E2M1X4),
-                rhs_scale=picked_plane[:],
-                start=True,
-                stop=True,
+            nc.scalar.copy(
+                out=w_dealt[:].rearrange("p (t c i) -> p c t i", t=PACK, i=4)[:, :, 2 * pair : 2 * pair + 2, :],
+                in_=w_raw[:].rearrange("p (c i t) -> p c t i", t=PACK, i=4)[:, :, 2 * pair : 2 * pair + 2, :],
             )
+
+        first = [[ps.tile([P, 2, J], F32, name="first%d%d" % (side, pair)) for pair in range(2)] for side in range(2)]
+        for side in range(2):
+            for t in range(PACK):
+                nc.tensor.matmul_mx(
+                    out=first[side][t // 2][:, t % 2, :],
+                    lhsT=w_dealt[:, t * P : (t + 1) * P].bitcast(E4M3X4),
+                    lhsT_scale=w_plane[:, t * P : (t + 1) * P],
+                    rhs=picked[:, side * J : (side + 1) * J].bitcast(E2M1X4),
+                    rhs_scale=picked_plane[:, side * J : (side + 1) * J],
+                    start=True,
+                    stop=True,
+                )
         second = [[ps.tile([P, H], F32, name="second%d%d" % (u, h)) for h in range(2)] for u in range(2)]
         for u in range(2):
             for h in range(2):
@@ -123,10 +124,11 @@ def tile_list_tied_fading_skip_bestoftwo_kernel(
                     stop=False,
                 )
 
-        moved = sb.tile([P, PACK, J], F32, name="moved")
+        moved_b = sb.tile([P, PACK, J], F32, name="moved_b")
         fade = sb.tile([P, PACK, J], F32, name="fade")
-        diff = [sb.tile([P, PACK, H], F32, name="diff0"), sb.tile([P, PACK, H], F32, name="diff1", tag="levels2")]
-        mag = [sb.tile([P, PACK, H], F32, name="mag%d" % u) for u in range(2)]
+        diff = sb.tile([P, 2, PACK, H], F32, name="diff", tag="levels2")
+        mag = sb.tile([P, PACK, H], F32, name="mag")
+        signed = sb.tile([P, PACK, H], F32, name="signed")
         hid = [sb.tile([P, PACK * H], BF16, name="hid%d" % u, align_bytes=64) for u in range(2)]
         hid_codes = [sb.tile([P, H], U32, name="hid_codes%d" % u, align_bytes=64) for u in range(2)]
         hid_plane = [sb.tile([P, H], U8, name="hid_plane%d" % u, align_bytes=64) for u in range(2)]
@@ -139,32 +141,35 @@ def tile_list_tied_fading_skip_bestoftwo_kernel(
         def look(t):
             nc.scalar.activation(out=fade[:, t, :], in_=levels[t][:].indirect(list3[:]), func=ACT.Exp, bias=neg_top[t][:])
 
-        def magnitude(u):
-            for t in range(PACK):
-                nc.vector.tensor_tensor(
-                    out=diff[u][:, t, :],
-                    in0=first[t][:, J + u * H : J + (u + 1) * H],
-                    in1=moved[:, t, u * H : (u + 1) * H],
-                    op=ALU.subtract,
-                )
-            nc.scalar.activation(out=mag[u][:], in_=diff[u][:], func=ACT.Abs)
-
-        for t in range(PACK):
-            nc.scalar.copy(out=moved[:, t, :], in_=first[t][:, 0:J])
-        for t in range(PACK - 1):
+        top(0)
+        look(0)
+        for pair in range(2):
+            nc.scalar.copy(out=moved_b[:, 2 * pair : 2 * pair + 2, :], in_=first[0][pair][:])
+        for t in range(1, PACK):
             top(t)
             look(t)
-        magnitude(0)
-        top(PACK - 1)
-        look(PACK - 1)
-        magnitude(1)
         for u in range(2):
-            nc.vector.tensor_tensor(
-                out=hid[u][:].rearrange("p (c i t) -> p c t i", t=PACK, i=2),
-                in0=mag[u][:].rearrange("p t (c i) -> p c t i", i=2),
-                in1=fade[:, :, u * H : (u + 1) * H].rearrange("p t (c i) -> p c t i", i=2),
-                op=ALU.mult,
-            )
+            for pair in range(2):
+                rows = slice(2 * pair, 2 * pair + 2)
+                cols = slice(u * H, (u + 1) * H)
+                nc.vector.tensor_tensor(
+                    out=diff[:, u, rows, :], in0=first[1][pair][:, :, cols], in1=moved_b[:, rows, cols], op=ALU.subtract
+                )
+        nc.scalar.activation(out=mag[:], in_=diff[:, 0, :, :], func=ACT.Abs)
+        for pair in range(2):
+            rows = slice(2 * pair, 2 * pair + 2)
+            nc.vector.tensor_tensor(out=signed[:, rows, :], in0=diff[:, 1, rows, :], in1=fade[:, rows, H:J], op=ALU.mult)
+        nc.vector.tensor_tensor(
+            out=hid[0][:].rearrange("p (c i t) -> p c t i", t=PACK, i=2),
+            in0=mag[:].rearrange("p t (c i) -> p c t i", i=2),
+            in1=fade[:, :, 0:H].rearrange("p t (c i) -> p c t i", i=2),
+            op=ALU.mult,
+        )
+        nc.scalar.activation(
+            out=hid[1][:].rearrange("p (c i t) -> p c t i", t=PACK, i=2),
+            in_=signed[:].rearrange("p t (c i) -> p c t i", i=2),
+            func=ACT.Abs,
+        )
         for u in range(2):
             nc.vector.quantize_mx(out=hid_codes[u][:].bitcast(E5M2X4), scales=hid_plane[u][:], in_=hid[u][:])
         whole = [sb.tile([P, J], F32, name="whole%d" % h) for h in range(2)]

@@ -45,11 +45,11 @@ def tile_list_tied_fading_skip_bestoftwo_kernel(
         list4 = sb.tile([P, E // 16], U16, name="list4")
         list5 = sb.tile([P, E // 16], U16, name="list5")
         x_words = sb.tile([P, T], U16, name="x_words")
-        x_plane = sb.tile([P, T], U8, name="x_plane")
+        x_plane = sb.tile([P, T], U8, name="x_plane", tag="x_plane", align_bytes=64)
         w_raw = sb.tile([P, R], U32, name="w_raw")
         w_raw_plane = sb.tile([P, R], U8, name="w_raw_plane")
         w_dealt = sb.tile([P, R], U32, name="w_dealt", align_bytes=64)
-        w_plane = sb.tile([P, R], U8, name="w_plane", align_bytes=64)
+        w_plane = sb.tile([P, R], U8, name="w_plane", tag="x_plane", align_bytes=64)
         ws_codes = sb.tile([P, N], U32, name="ws_codes", align_bytes=64)
         wb_codes = sb.tile([P, 2 * N], U8, name="wb_codes", align_bytes=64)
         ws_plane = sb.tile([P, N], U8, name="ws_plane", align_bytes=64)

from contextlib import ExitStack

import concourse.mybir as mybir

K, T, J, R, Q, N, E = 512, 2048, 256, 512, 1024, 256, 128
FLOPS = 2 * K * R * J * 2 + 2 * R * N * J + 2 * K * N * J

F32 = mybir.dt.float32
BF16 = mybir.dt.bfloat16
I32 = mybir.dt.int32
U32 = mybir.dt.uint32
U16 = mybir.dt.uint16
U8 = mybir.dt.uint8
E2M1X4 = mybir.dt.float4_e2m1fn_x4
E4M3X4 = mybir.dt.float8_e4m3fn_x4
E5M2X4 = mybir.dt.float8_e5m2_x4
ALU = mybir.AluOpType
ACT = mybir.ActivationFunctionType

P = 128
PACK = 4
H = J // 2


def load_scale_rows(queue, plane, rows, quads=(0, 1, 2, 3)):
    for quad in quads:
        queue.dma_start(
            out=plane[32 * quad : 32 * quad + 4, :].bitcast(I32),
            in_=rows[0, 4 * quad : 4 * quad + 4, :].bitcast(I32),
        )


def tile_list_tied_fading_skip_bestoftwo_kernel(
    tc, xt_words, xt_scales, w_words, w_scales, ta, wb_words, wb_scales, ws_words, ws_scales,
    offs, offs2, offs3, offs4, offs5, out,
):
    nc = tc.nc
    with ExitStack() as ctx:
        sb = ctx.enter_context(tc.tile_pool(name="sb", bufs=1))
        ps = ctx.enter_context(tc.psum_pool(name="ps", bufs=1))

        list1 = sb.tile([P, J // 16], U16, name="list1")
        list2 = sb.tile([P, J // 16], U16, name="list2")
        list3 = sb.tile([P, J // 16], U16, name="list3")
        list4 = sb.tile([P, E // 16], U16, name="list4")
        list5 = sb.tile([P, E // 16], U16, name="list5")
        x_words = sb.tile([P, T], U16, name="x_words")
        x_plane = sb.tile([P, T], U8, name="x_plane", tag="x_plane", align_bytes=64)
        w_raw = sb.tile([P, R], U32, name="w_raw")
        w_raw_plane = sb.tile([P, R], U8, name="w_raw_plane")
        w_dealt = sb.tile([P, R], U32, name="w_dealt", align_bytes=64)
        w_plane = sb.tile([P, R], U8, name="w_plane", tag="x_plane", align_bytes=64)
        ws_codes = sb.tile([P, N], U32, name="ws_codes", align_bytes=64)
        wb_codes = sb.tile([P, 2 * N], U8, name="wb_codes", align_bytes=64)
        ws_plane = sb.tile([P, N], U8, name="ws_plane", align_bytes=64)
        wb_plane = sb.tile([P, N], U8, name="wb_plane", align_bytes=64)
        levels = [sb.tile([P, Q], F32, name="levels%d" % t, tag="levels%d" % t) for t in range(PACK)]
        neg_top = [sb.tile([P, 1], F32, name="neg_top%d" % t) for t in range(PACK)]
        picked = sb.tile([P, 2 * J], U16, name="picked", align_bytes=64)
        picked_plane = sb.tile([P, 2 * J], U8, name="picked_plane", align_bytes=64)

        nc.vector.memset(x_plane[:, 0 : T // 2].bitcast(I32), 0)
        nc.gpsimd.memset(x_plane[:, T // 2 : T].bitcast(I32), 0)
        nc.vector.memset(w_raw_plane[:].bitcast(I32), 0)
        nc.gpsimd.memset(ws_plane[:].bitcast(I32), 0)
        nc.gpsimd.memset(wb_plane[:].bitcast(I32), 0)

        ta_rows = ta.rearrange("(p t) q -> p t q", t=PACK)
        nc.sync.dma_start(list2[:], offs2)
        nc.sync.dma_start(out=x_words[:].bitcast(I32), in_=xt_words[0].bitcast(I32))
        nc.sync.dma_start(list1[:], offs)
        load_scale_rows(nc.sync, x_plane, xt_scales)
        nc.sync.dma_start(out=w_raw[:].bitcast(I32), in_=w_words[0].rearrange("p n t -> p (n t)").bitcast(I32))
        nc.sync.dma_start(out=levels[0][:], in_=ta_rows[:, 0, :])
        nc.sync.dma_start(list3[:], offs3)
        load_scale_rows(nc.sync, w_raw_plane, w_scales)
        nc.sync.dma_start(out=levels[1][:], in_=ta_rows[:, 1, :])
        for t in range(2, PACK):
            nc.sync.dma_start(out=levels[t][:], in_=ta_rows[:, t, :])
        load_scale_rows(nc.sync, ws_plane, ws_scales)
        nc.sync.dma_start(out=ws_codes[:].bitcast(I32), in_=ws_words[0].rearrange("p n t -> p (n t)").bitcast(I32))
        nc.sync.dma_start(out=wb_codes[:].bitcast(I32), in_=wb_words[0].bitcast(I32))
        load_scale_rows(nc.sync, wb_plane, wb_scales)
        nc.sync.dma_start(list4[:], offs4)
        nc.sync.dma_start(list5[:], offs5)

        nc.vector.tensor_copy(picked[:, 0:J], x_words[:].indirect(list2[:]))
        nc.vector.tensor_copy(picked[:, J : 2 * J], x_words[:].indirect(list1[:]))
        nc.vector.tensor_copy(picked_plane[:, 0:J], x_plane[:].indirect(list2[:]))
        nc.vector.tensor_copy(picked_plane[:, J : 2 * J], x_plane[:].indirect(list1[:]))

        for pair in range(2):
            nc.gpsimd.tensor_copy(
                out=w_plane[:].rearrange("p (t c i) -> p c t i", t=PACK, i=16)[:, :, 2 * pair : 2 * pair + 2, :],
                in_=w_raw_plane[:].rearrange("p (c i t) -> p c t i", t=PACK, i=16)[:, :, 2 * pair : 2 * pair + 2, :],
            )
            nc.scalar.copy(
                out=w_dealt[:].rearrange("p (t c i) -> p c t i", t=PACK, i=4)[:, :, 2 * pair : 2 * pair + 2, :],
                in_=w_raw[:].rearrange("p (c i t) -> p c t i", t=PACK, i=4)[:, :, 2 * pair : 2 * pair + 2, :],
            )

        first = [[ps.tile([P, 2, J], F32, name="first%d%d" % (side, pair)) for pair in range(2)] for side in range(2)]
        for side in range(2):
            for t in range(PACK):
                nc.tensor.matmul_mx(
                    out=first[side][t // 2][:, t % 2, :],
                    lhsT=w_dealt[:, t * P : (t + 1) * P].bitcast(E4M3X4),
                    lhsT_scale=w_plane[:, t * P : (t + 1) * P],
                    rhs=picked[:, side * J : (side + 1) * J].bitcast(E2M1X4),
                    rhs_scale=picked_plane[:, side * J : (side + 1) * J],
                    start=True,
                    stop=True,
                )
        second = [[ps.tile([P, H], F32, name="second%d%d" % (u, h)) for h in range(2)] for u in range(2)]
        for u in range(2):
            for h in range(2):
                nc.tensor.matmul_mx(
                    out=second[u][h][:],
                    lhsT=ws_codes[:, h * P : (h + 1) * P].bitcast(E4M3X4),
                    lhsT_scale=ws_plane[:, h * P : (h + 1) * P],
                    rhs=picked[:, J + u * H : J + (u + 1) * H].bitcast(E2M1X4),
                    rhs_scale=picked_plane[:, J + u * H : J + (u + 1) * H],
                    start=True,
                    stop=False,
                )

        moved_b = sb.tile([P, PACK, J], F32, name="moved_b")
        fade = sb.tile([P, PACK, J], F32, name="fade")
        diff = sb.tile([P, 2, PACK, H], F32, name="diff", tag="levels2")
        mag = sb.tile([P, PACK, H], F32, name="mag")
        signed = sb.tile([P, PACK, H], F32, name="signed")
        hid = [sb.tile([P, PACK * H], BF16, name="hid%d" % u, align_bytes=64) for u in range(2)]
        hid_codes = [sb.tile([P, H], U32, name="hid_codes%d" % u, align_bytes=64) for u in range(2)]
        hid_plane = [sb.tile([P, H], U8, name="hid_plane%d" % u, align_bytes=64) for u in range(2)]

        def top(t):
            nc.vector.tensor_reduce(
                out=neg_top[t][:], in_=levels[t][:], axis=mybir.AxisListType.X, op=ALU.max, negate=True
            )

        def look(t):
            nc.scalar.activation(out=fade[:, t, :], in_=levels[t][:].indirect(list3[:]), func=ACT.Exp, bias=neg_top[t][:])

        top(0)
        look(0)
        for pair in range(2):
            nc.scalar.copy(out=moved_b[:, 2 * pair : 2 * pair + 2, :], in_=first[0][pair][:])
        for t in range(1, PACK):
            top(t)
            look(t)
        for u in range(2):
            for pair in range(2):
                rows = slice(2 * pair, 2 * pair + 2)
                cols = slice(u * H, (u + 1) * H)
                nc.vector.tensor_tensor(
                    out=diff[:, u, rows, :], in0=first[1][pair][:, :, cols], in1=moved_b[:, rows, cols], op=ALU.subtract
                )
        nc.scalar.activation(out=mag[:], in_=diff[:, 0, :, :], func=ACT.Abs)
        for pair in range(2):
            rows = slice(2 * pair, 2 * pair + 2)
            nc.vector.tensor_tensor(out=signed[:, rows, :], in0=diff[:, 1, rows, :], in1=fade[:, rows, H:J], op=ALU.mult)
        nc.vector.tensor_tensor(
            out=hid[0][:].rearrange("p (c i t) -> p c t i", t=PACK, i=2),
            in0=mag[:].rearrange("p t (c i) -> p c t i", i=2),
            in1=fade[:, :, 0:H].rearrange("p t (c i) -> p c t i", i=2),
            op=ALU.mult,
        )
        nc.scalar.activation(
            out=hid[1][:].rearrange("p (c i t) -> p c t i", t=PACK, i=2),
            in_=signed[:].rearrange("p t (c i) -> p c t i", i=2),
            func=ACT.Abs,
        )
        for u in range(2):
            nc.vector.quantize_mx(out=hid_codes[u][:].bitcast(E5M2X4), scales=hid_plane[u][:], in_=hid[u][:])
        whole = [sb.tile([P, J], F32, name="whole%d" % h) for h in range(2)]
        for u in range(2):
            for h in range(2):
                nc.tensor.matmul_mx(
                    out=second[u][h][:],
                    lhsT=wb_codes[:, 2 * h * P : 2 * (h + 1) * P].bitcast(E2M1X4),
                    lhsT_scale=wb_plane[:, h * P : (h + 1) * P],
                    rhs=hid_codes[u][:].bitcast(E5M2X4),
                    rhs_scale=hid_plane[u][:],
                    start=False,
                    stop=True,
                )
        for h in range(2):
            nc.scalar.copy(out=whole[h][:, 0:H], in_=second[0][h][:])
        nc.vector.tensor_copy(out=whole[0][:, H:J], in_=second[1][0][:])
        nc.scalar.copy(out=whole[1][:, H:J], in_=second[1][1][:])

        left = [sb.tile([P, E], F32, name="left%d" % h) for h in range(2)]
        right = [sb.tile([P, E], F32, name="right%d" % h) for h in range(2)]
        best = [sb.tile([P, E], F32, name="best%d" % h) for h in range(2)]
        for h in range(2):
            nc.vector.tensor_copy(left[h][:], whole[h][:].indirect(list4[:]))
            nc.scalar.activation(out=right[h][:], in_=whole[h][:].indirect(list5[:]), func=ACT.Copy)
        for h in range(2):
            nc.vector.tensor_tensor(out=best[h][:], in0=left[h][:], in1=right[h][:], op=ALU.max)
            (nc.sync, nc.scalar)[h].dma_start(out=out[h * P : (h + 1) * P, :], in_=best[h][:])
